import numpy as np
import ml_dtypes


def mxq(x, axis, fmt="e4m3"):
    dtype, down = {"e4m3": (ml_dtypes.float8_e4m3fn, 7), "e5m2": (ml_dtypes.float8_e5m2, 14)}[fmt]
    v = np.moveaxis(np.asarray(x, np.float32).astype(ml_dtypes.bfloat16).astype(np.float64), axis, -1)
    blocks = v.reshape(v.shape[:-1] + (-1, 32))
    amax = np.abs(blocks).max(-1, keepdims=True)
    byte = np.maximum(np.where(amax > 0, np.frexp(amax)[1] - 1 + 127, 0) - down, 1)
    scale = np.exp2(byte - 127.0)
    codes = (blocks / scale).astype(np.float32).astype(dtype).astype(np.float64)
    return np.moveaxis((codes * scale).reshape(v.shape), -1, axis)


WIDE = False


def mx_kscale(k):
    if not WIDE:
        return np.ones(k)
    levels = np.array([10, -10, 5, -5, 0])
    if k % 512:
        return np.exp2(np.random.permutation(np.resize(levels, k // 32))).repeat(32)
    a = np.empty((k // 512, 16))
    for p in range(k // 512):
        a[p, :8] = np.random.permutation(np.resize(levels, 8))
        for g in range(8):
            far = levels[np.abs(levels - a[p, g]) >= 10]
            a[p, g + 8] = far[np.random.randint(len(far))]
    return np.exp2(a.ravel()).repeat(32)


def f64(x):
    return np.asarray(x).astype(np.float64)


def striped(idx):
    return np.tile(idx.reshape(-1, 16).T, (8, 1)).astype(np.uint16)


def unstriped(offs):
    return offs[:16].T.reshape(-1).astype(np.int64)


def striped8(idx):
    return np.concatenate([x.reshape(-1, 16).T for x in idx]).astype(np.uint16)


def runs(offs, k):
    lists = np.stack([offs[16 * r : 16 * r + 16].T.reshape(-1) for r in range(8)]).astype(np.int64)
    return lists[np.arange(k) % 512 // 64]


def pack_weight(w):
    k, n = w.shape
    w = f64(np.asarray(w, np.float32).astype(ml_dtypes.bfloat16)).reshape(k // 32, 32, n)
    amax = np.abs(w).max(1)
    byte = np.clip(np.where(amax > 0, np.frexp(amax)[1] - 1 + 127 - 7, 1), 1, 254)
    scaled = (w * np.exp2(127.0 - byte)[:, None, :]).reshape(k, n).astype(np.float32)
    words = np.ascontiguousarray(scaled.reshape(k // 512, 128, 4, n).transpose(0, 1, 3, 2)).astype(ml_dtypes.float8_e4m3fn).view(np.uint8)
    return words, np.ascontiguousarray(byte.astype(np.uint8).reshape(k // 512, 16, n))


def unpack_weight(words, scales):
    g, p, n, _ = words.shape
    vals = np.ascontiguousarray(words).view(ml_dtypes.float8_e4m3fn).astype(np.float64) * np.repeat(np.exp2(scales.astype(np.float64) - 127.0), 8, axis=1)[..., None]
    return vals.transpose(0, 1, 3, 2).reshape(g * 512, n)


K, T, S, N, G, H, J = 512, 2048, 256, 512, 2048, 512, 512


def setup_inputs():
    n = np.random.standard_normal
    s = mx_kscale(K)[:, None]
    u = mx_kscale(K)
    packed_xT = pack_weight(n((K, T)) * s)
    packed_dT = pack_weight(n((K, G)) / s)
    return {
        "x_words": packed_xT[0],
        "x_scales": packed_xT[1],
        "d_words": packed_dT[0],
        "d_scales": packed_dT[1],
        "gn": (np.random.uniform(0.5, 1.5, (H, 1)) * u[:, None]).astype(np.float32),
        "w1": (n((H, N)) / np.sqrt(2 * H) / u[:, None]).astype(np.float32),
        "w2": (n((K, N)) / np.sqrt(2 * K) / s).astype(np.float32),
        "offs": striped(np.random.permutation(T)[:S]),
        "k1": striped8(np.random.randint(0, G, (8, H))),
        "n1": striped(np.random.permutation(S)),
        "n2": striped(np.random.permutation(S)),
        "two": striped(np.random.permutation(T)[:S]),
        "n3": striped(np.random.randint(0, S, J)),
        "n4": striped(np.random.permutation(S)),
    }


def reference(x_words, x_scales, d_words, d_scales, gn, w1, w2, offs, k1, n1, n2, two, n3, n4):
    d_k1 = unpack_weight(d_words, d_scales)[np.arange(K)[:, None], runs(k1, K)]
    xq = unpack_weight(x_words, x_scales)[:, unstriped(offs)]
    s = 0.0625 * (d_k1.T @ xq)
    z = f64(gn) * (s - (np.minimum(s[:, unstriped(n1)], s[:, unstriped(n2)])))
    x_two = unpack_weight(x_words, x_scales)[:, unstriped(two)]
    h = mxq(f64(w1), 0, "e4m3").T @ mxq(z, 0, "e4m3") + mxq(f64(w2), 0, "e4m3").T @ x_two
    mb = h[:, unstriped(n3)]
    mx = mb.reshape(N, S, 2).max(axis=2)
    st = h - mx
    return np.maximum(st, st[:, unstriped(n4)])

@@ -1,0 +1,215 @@
+from contextlib import ExitStack
+
+import concourse.mybir as mybir
+
+F32 = mybir.dt.float32
+BF16 = mybir.dt.bfloat16
+I32 = mybir.dt.int32
+U32 = mybir.dt.uint32
+U16 = mybir.dt.uint16
+U8 = mybir.dt.uint8
+FP8X4 = mybir.dt.float8_e4m3fn_x4
+ALU = mybir.AluOpType
+COPY = mybir.ActivationFunctionType.Copy
+
+P = 128
+PACK = 4
+T = 2048
+S = 256
+H = 512
+N = 512
+J = 512
+FLOPS = 3 * 2 * 512 * 512 * 256
+
+
+def tile_picked_kmixunderghopm_none_p_kernel(tc, x_words, x_scales, d_words, d_scales, gn, w1, w2, offs, k1, n1, n2, two, n3, n4, out):
+    nc = tc.nc
+    with ExitStack() as ctx:
+        lists = ctx.enter_context(tc.tile_pool(name="lists", bufs=1))
+        pool = ctx.enter_context(tc.tile_pool(name="pool", bufs=1))
+        psum = ctx.enter_context(tc.psum_pool(name="psum", bufs=1))
+
+        def load_list(src, name):
+            tile = lists.tile(list(src.shape), U16, name=name)
+            nc.sync.dma_start(tile[:], src)
+            return tile
+
+        x_sc = pool.tile([P, T], U8, name="x_sc", tag="x_sc", align_bytes=64)
+        nc.vector.memset(x_sc[:].bitcast(I32), 0)
+        S_WIN, H_WIN, ST_WIN = 384, J + 16, S + 16
+        s = pool.tile([P, (PACK - 1) * S + S_WIN], F32, name="s")
+        h = [pool.tile([P, H_WIN], F32, name="h%d" % m) for m in range(4)]
+        st = [pool.tile([P, ST_WIN], F32, name="st%d" % m) for m in range(4)]
+        nc.vector.memset(s[:, PACK * S:], 0.0)
+        for m in range(4):
+            nc.vector.memset(h[m][:, S:], 0.0)
+            nc.vector.memset(st[m][:, S:], 0.0)
+
+        k1_t = load_list(k1, "k1")
+        d_sc = pool.tile([P, T], U8, name="d_sc", tag="d_sc", align_bytes=64)
+        for e in range(2):
+            rows = d_scales[0, e:16:2, :].bitcast(I32)
+            nc.sync.dma_start(d_sc[e:P:2, :].bitcast(I32), rows.unsqueeze(1).to_broadcast([8, 8, T // 4]))
+        offs_t = load_list(offs, "offs")
+        two_t = load_list(two, "two")
+        n1_t = load_list(n1, "n1")
+        n2_t = load_list(n2, "n2")
+        d_w = pool.tile([P, T], U32, name="d_w", tag="d_w", align_bytes=64)
+        nc.sync.dma_start(d_w[:].bitcast(I32), d_words[0].rearrange("p n t -> p (n t)").bitcast(I32))
+        for a in range(4):
+            nc.scalar.dma_start(x_sc[a:P:32, :].bitcast(I32), x_scales[0, a:16:4, :].bitcast(I32))
+        x_w = pool.tile([P, T], U32, name="x_w", tag="d_sc", align_bytes=64)
+        nc.sync.dma_start(x_w[:].bitcast(I32), x_words[0].rearrange("p n t -> p (n t)").bitcast(I32))
+        n3_t = load_list(n3, "n3")
+        n4_t = load_list(n4, "n4")
+
+        dk_sc = pool.tile([P, H], U8, name="dk_sc", tag="dk_sc", align_bytes=64)
+        nc.vector.tensor_copy(dk_sc[:], d_sc[:].indirect(k1_t[:]))
+        key_sc = pool.tile([P, H], U8, name="key_sc", align_bytes=64)
+        nc.vector.tensor_copy(key_sc[:].rearrange("p (t m) -> p m t", t=PACK), dk_sc[:].rearrange("p (m t) -> p m t", t=PACK))
+        for e in range(2):
+            nc.scalar.dma_start(key_sc[2 + e:P:32, :].bitcast(I32), key_sc[16 + e:P:32, :].bitcast(I32))
+
+        xq_sc = pool.tile([P, S], U8, name="xq_sc", align_bytes=64)
+        x2_sc = pool.tile([P, S], U8, name="x2_sc", align_bytes=64)
+        dk_w = pool.tile([P, H], U32, name="dk_w", tag="dk_w", align_bytes=64)
+        key_w = pool.tile([P, H], U32, name="key_w", align_bytes=64)
+        xq_w = pool.tile([P, S], U32, name="xq_w", align_bytes=64)
+        x2_w = pool.tile([P, S], U32, name="x2_w", align_bytes=64)
+        nc.vector.tensor_copy(xq_sc[:], x_sc[:].indirect(offs_t[:]))
+        nc.vector.tensor_copy(dk_w[:], d_w[:].indirect(k1_t[:]))
+        nc.vector.tensor_copy(key_w[:].rearrange("p (t m) -> p m t", t=PACK), dk_w[:].rearrange("p (m t) -> p m t", t=PACK))
+        nc.vector.tensor_copy(x2_sc[:], x_sc[:].indirect(two_t[:]))
+        nc.vector.tensor_copy(xq_w[:], x_w[:].indirect(offs_t[:]))
+
+        g = pool.tile([P, PACK], F32, name="g", tag="dk_sc", align_bytes=64)
+        nc.sync.dma_start(g[:], gn.rearrange("(p t) o -> p (t o)", t=PACK))
+        HALF = N // 2
+        raws = {}
+        after = {("w2", 0): "d_w", ("w1", 0): "dk_w", ("w2", 1): "x_sc", ("w1", 1): "d_sc"}
+        for hf in range(2):
+            for name, w in (("w2", w2), ("w1", w1)):
+                raw = pool.tile([P, PACK, HALF], F32, name="raw_%s_%d" % (name, hf), tag=after[(name, hf)], align_bytes=64)
+                nc.sync.dma_start(raw[:], w.rearrange("(p j) n -> p j n", j=PACK)[:, :, hf * HALF:(hf + 1) * HALF])
+                raws[(name, hf)] = raw
+
+        s_ps = [psum.tile([P, S], F32, name="s_ps%d" % t) for t in range(PACK)]
+        for t in (3, 2, 1, 0):
+            cols = slice(t * P, (t + 1) * P)
+            nc.tensor.matmul_mx(out=s_ps[t][:], lhsT=key_w[:, cols].bitcast(FP8X4), lhsT_scale=key_sc[:, cols],
+                                rhs=xq_w[:].bitcast(FP8X4), rhs_scale=xq_sc[:], start=True, stop=True)
+        nc.scalar.activation(s[:, 3 * S:4 * S], s_ps[3][:], COPY, scale=0.0625)
+        nc.vector.tensor_scalar(s[:, 2 * S:3 * S], s_ps[2][:], 0.0625, None, ALU.mult)
+        nc.vector.tensor_copy(x2_w[:], x_w[:].indirect(two_t[:]))
+        for t in (1, 0):
+            nc.vector.tensor_scalar(s[:, t * S:(t + 1) * S], s_ps[t][:], 0.0625, None, ALU.mult)
+        s3 = s[:, :PACK * S].rearrange("p (t j) -> p t j", t=PACK)
+
+        w_bf, w_q, w_sc = {}, {}, {}
+
+        def cast_w(name, m, copy, tag=None):
+            key = (name, m)
+            grouped = pool.tile([P, P * PACK], BF16, name="bf_%s_%d" % key, tag=tag or "bf_%s_%d" % key, align_bytes=64)
+            dst = grouped[:].rearrange("p (c i t) -> p c t i", i=4, t=PACK)
+            src = raws[(name, m // 2)][:, :, (m % 2) * P:(m % 2 + 1) * P].rearrange("p t (c i) -> p c t i", i=4)
+            copy(dst, src)
+            w_bf[key] = grouped
+
+        def quant_w(name, m):
+            key = (name, m)
+            w_q[key] = pool.tile([P, P], U32, name="q_%s_%d" % key, align_bytes=64)
+            w_sc[key] = pool.tile([P, P], U8, name="sc_%s_%d" % key, align_bytes=64)
+            nc.vector.quantize_mx(out=w_q[key][:].bitcast(FP8X4), scales=w_sc[key][:], in_=w_bf[key][:])
+
+        z_bf = pool.tile([P, S * PACK], BF16, name="z_bf", align_bytes=64)
+        z_q = pool.tile([P, S], U32, name="z_q", align_bytes=64)
+        z_sc = pool.tile([P, S], U8, name="z_sc", align_bytes=64)
+
+        tiles = {}
+        for c0, c1 in ((0, 192), (192, 256)):
+            for nm in ("a", "b", "low", "dif"):
+                tiles[(nm, c0)] = pool.tile([P, PACK, c1 - c0], F32, name="%s%d" % (nm, c0), tag="%s%d" % (nm, c0), align_bytes=64)
+
+        def fetch(c0, c1, t0, t1):
+            a, b, low, dif = (tiles[(nm, c0)] for nm in ("a", "b", "low", "dif"))
+            for t in range(t1 - 1, t0 - 1, -1):
+                win = s[:, t * S:t * S + S_WIN]
+                nc.scalar.activation(a[:, t, :], win.indirect(n1_t[:, c0 // 16:c1 // 16]), COPY)
+                nc.scalar.activation(b[:, t, :], win.indirect(n2_t[:, c0 // 16:c1 // 16]), COPY)
+            nc.vector.tensor_tensor(low[:, t0:t1, :], a[:, t0:t1, :], b[:, t0:t1, :], ALU.min)
+            nc.vector.tensor_tensor(dif[:, t0:t1, :], s3[:, t0:t1, c0:c1], low[:, t0:t1, :], ALU.subtract)
+
+        def gain(c0, c1):
+            nc.vector.tensor_tensor(
+                z_bf[:, c0 * PACK:c1 * PACK].rearrange("p (c i t) -> p c t i", i=4, t=PACK),
+                tiles[("dif", c0)][:].rearrange("p t (c i) -> p c t i", i=4),
+                g[:].unsqueeze(1).unsqueeze(3).to_broadcast([P, (c1 - c0) // 4, PACK, 4]), ALU.mult)
+
+        def quant_z(c0, c1):
+            nc.vector.quantize_mx(out=z_q[:, c0:c1].bitcast(FP8X4), scales=z_sc[:, c0:c1], in_=z_bf[:, c0 * PACK:c1 * PACK])
+
+        cast_w("w2", 0, nc.vector.tensor_copy)
+        fetch(0, 192, 2, 4)
+        quant_w("w2", 0)
+        cast_w("w1", 0, nc.vector.tensor_copy)
+        fetch(0, 192, 1, 2)
+        quant_w("w1", 0)
+        fetch(0, 192, 0, 1)
+        gain(0, 192)
+        fetch(192, 256, 1, 4)
+        quant_z(0, 128)
+        quant_z(128, 192)
+        fetch(192, 256, 0, 1)
+        gain(192, 256)
+        quant_z(192, 256)
+        cast_w("w2", 1, nc.scalar.copy, "a0")
+        cast_w("w1", 1, nc.scalar.copy, "b0")
+
+        h_ps = [psum.tile([P, S], F32, name="h_ps%d" % m) for m in range(4)]
+
+        def product(m, copy):
+            nc.tensor.matmul_mx(out=h_ps[m][:], lhsT=w_q[("w2", m)][:].bitcast(FP8X4), lhsT_scale=w_sc[("w2", m)][:],
+                                rhs=x2_w[:].bitcast(FP8X4), rhs_scale=x2_sc[:], start=True, stop=False)
+            nc.tensor.matmul_mx(out=h_ps[m][:], lhsT=w_q[("w1", m)][:].bitcast(FP8X4), lhsT_scale=w_sc[("w1", m)][:],
+                                rhs=z_q[:].bitcast(FP8X4), rhs_scale=z_sc[:], start=False, stop=True)
+            copy(h[m][:, :S], h_ps[m][:])
+
+        def members(m, pieces):
+            mb = pool.tile([P, J], F32, name="mb%d" % m)
+            mx = pool.tile([P, S], F32, name="mx%d" % m)
+            for c0, c1 in pieces:
+                nc.scalar.activation(mb[:, 2 * c0:2 * c1], h[m][:].indirect(n3_t[:, c0 // 8:c1 // 8]), COPY)
+                nc.vector.tensor_tensor(mx[:, c0:c1], mb[:, 2 * c0:2 * c1:2], mb[:, 2 * c0 + 1:2 * c1:2], ALU.max)
+                nc.vector.tensor_tensor(st[m][:, c0:c1], h[m][:, c0:c1], mx[:, c0:c1], ALU.subtract)
+
+        def finish(m, pieces):
+            for c0, c1 in pieces:
+                far = pool.tile([P, c1 - c0], F32, name="far%d_%d" % (m, c0))
+                res = pool.tile([P, c1 - c0], F32, name="res%d_%d" % (m, c0))
+                nc.scalar.activation(far[:], st[m][:].indirect(n4_t[:, c0 // 16:c1 // 16]), COPY)
+                nc.vector.tensor_tensor(res[:], st[m][:, c0:c1], far[:], ALU.max)
+                nc.sync.dma_start(out[m * P:(m + 1) * P, c0:c1], res[:])
+
+        def weights(m):
+            cast_w("w2", m, nc.vector.tensor_copy)
+            cast_w("w1", m, nc.vector.tensor_copy)
+            quant_w("w2", m)
+            quant_w("w1", m)
+
+        whole = [(0, S)]
+        product(0, nc.scalar.copy)
+        quant_w("w2", 1)
+        quant_w("w1", 1)
+        product(1, nc.vector.tensor_copy)
+        weights(2)
+        members(0, whole)
+        product(2, nc.vector.tensor_copy)
+        weights(3)
+        members(1, whole)
+        product(3, nc.vector.tensor_copy)
+        finish(0, whole)
+        members(2, whole)
+        finish(1, whole)
+        members(3, [(0, 192), (192, 256)])
+        finish(2, whole)
+        finish(3, [(0, 192), (192, 256)])

@@ -27,6 +27,7 @@ def tile_picked_kmixunderghopm_none_p_kernel(tc, x_words, x_scales, d_words, d_s
     with ExitStack() as ctx:
         lists = ctx.enter_context(tc.tile_pool(name="lists", bufs=1))
         pool = ctx.enter_context(tc.tile_pool(name="pool", bufs=1))
+        turn = ctx.enter_context(tc.tile_pool(name="turn", bufs=1))
         psum = ctx.enter_context(tc.psum_pool(name="psum", bufs=1))
 
         def load_list(src, name):
@@ -34,8 +35,12 @@ def tile_picked_kmixunderghopm_none_p_kernel(tc, x_words, x_scales, d_words, d_s
             nc.sync.dma_start(tile[:], src)
             return tile
 
-        x_sc = pool.tile([P, T], U8, name="x_sc", tag="x_sc", align_bytes=64)
-        nc.vector.memset(x_sc[:].bitcast(I32), 0)
+        d_sc = pool.tile([P, T], U8, name="d_sc", align_bytes=64)
+        x_sc = pool.tile([P, T], U8, name="x_sc", align_bytes=64)
+        nc.vector.memset(d_sc[:, :T // 2].bitcast(I32), 0)
+        nc.gpsimd.memset(d_sc[:, T // 2:].bitcast(I32), 0)
+        nc.vector.memset(x_sc[:, :T // 2].bitcast(I32), 0)
+        nc.gpsimd.memset(x_sc[:, T // 2:].bitcast(I32), 0)
         S_WIN, H_WIN, ST_WIN = 384, J + 16, S + 16
         s = pool.tile([P, (PACK - 1) * S + S_WIN], F32, name="s")
         h = [pool.tile([P, H_WIN], F32, name="h%d" % m) for m in range(4)]
@@ -46,52 +51,71 @@ def tile_picked_kmixunderghopm_none_p_kernel(tc, x_words, x_scales, d_words, d_s
             nc.vector.memset(st[m][:, S:], 0.0)
 
         k1_t = load_list(k1, "k1")
-        d_sc = pool.tile([P, T], U8, name="d_sc", tag="d_sc", align_bytes=64)
-        for e in range(2):
-            rows = d_scales[0, e:16:2, :].bitcast(I32)
-            nc.sync.dma_start(d_sc[e:P:2, :].bitcast(I32), rows.unsqueeze(1).to_broadcast([8, 8, T // 4]))
         offs_t = load_list(offs, "offs")
+        nc.sync.dma_start(d_sc[0:P:8, :].bitcast(I32), d_scales[0].bitcast(I32))
+        for a in range(4):
+            nc.sync.dma_start(x_sc[a:P:32, :].bitcast(I32), x_scales[0, a:16:4, :].bitcast(I32))
+        d_w = pool.tile([P, T], U32, name="d_w", align_bytes=64)
+        nc.sync.dma_start(d_w[:].bitcast(I32), d_words[0].rearrange("p n t -> p (n t)").bitcast(I32))
         two_t = load_list(two, "two")
+        HALF = N // 2
+        raws = {}
+
+        def load_weights(name, w, hf):
+            raw = pool.tile([P, PACK, HALF], F32, name="raw_%s_%d" % (name, hf))
+            nc.sync.dma_start(raw[:], w.rearrange("(p j) n -> p j n", j=PACK)[:, :, hf * HALF:(hf + 1) * HALF])
+            raws[(name, hf)] = raw
+
+        x_w = pool.tile([P, T], U32, name="x_w", tag="x_w", align_bytes=64)
+        nc.sync.dma_start(x_w[:].bitcast(I32), x_words[0].rearrange("p n t -> p (n t)").bitcast(I32))
+        g = pool.tile([P, PACK], F32, name="g")
+        nc.sync.dma_start(g[:], gn.rearrange("(p t) o -> p (t o)", t=PACK))
         n1_t = load_list(n1, "n1")
         n2_t = load_list(n2, "n2")
-        d_w = pool.tile([P, T], U32, name="d_w", tag="d_w", align_bytes=64)
-        nc.sync.dma_start(d_w[:].bitcast(I32), d_words[0].rearrange("p n t -> p (n t)").bitcast(I32))
-        for a in range(4):
-            nc.scalar.dma_start(x_sc[a:P:32, :].bitcast(I32), x_scales[0, a:16:4, :].bitcast(I32))
-        x_w = pool.tile([P, T], U32, name="x_w", tag="d_sc", align_bytes=64)
-        nc.sync.dma_start(x_w[:].bitcast(I32), x_words[0].rearrange("p n t -> p (n t)").bitcast(I32))
-        n3_t = load_list(n3, "n3")
-        n4_t = load_list(n4, "n4")
 
-        dk_sc = pool.tile([P, H], U8, name="dk_sc", tag="dk_sc", align_bytes=64)
+        dk_sc = pool.tile([P, H], U8, name="dk_sc", align_bytes=64)
         nc.vector.tensor_copy(dk_sc[:], d_sc[:].indirect(k1_t[:]))
         key_sc = pool.tile([P, H], U8, name="key_sc", align_bytes=64)
         nc.vector.tensor_copy(key_sc[:].rearrange("p (t m) -> p m t", t=PACK), dk_sc[:].rearrange("p (m t) -> p m t", t=PACK))
-        for e in range(2):
-            nc.scalar.dma_start(key_sc[2 + e:P:32, :].bitcast(I32), key_sc[16 + e:P:32, :].bitcast(I32))
+        for a in range(1, 4):
+            nc.sync.dma_start(key_sc[a:P:32, :].bitcast(I32), key_sc[8 * a:P:32, :].bitcast(I32))
+        load_weights("w2", w2, 0)
+        load_weights("w1", w1, 0)
+        load_weights("w2", w2, 1)
+        load_weights("w1", w1, 1)
+        n3_t = load_list(n3, "n3")
+        n4_t = load_list(n4, "n4")
 
         xq_sc = pool.tile([P, S], U8, name="xq_sc", align_bytes=64)
         x2_sc = pool.tile([P, S], U8, name="x2_sc", align_bytes=64)
-        dk_w = pool.tile([P, H], U32, name="dk_w", tag="dk_w", align_bytes=64)
+        dk_w = pool.tile([P, H], U32, name="dk_w", align_bytes=64)
         key_w = pool.tile([P, H], U32, name="key_w", align_bytes=64)
         xq_w = pool.tile([P, S], U32, name="xq_w", align_bytes=64)
         x2_w = pool.tile([P, S], U32, name="x2_w", align_bytes=64)
         nc.vector.tensor_copy(xq_sc[:], x_sc[:].indirect(offs_t[:]))
         nc.vector.tensor_copy(dk_w[:], d_w[:].indirect(k1_t[:]))
-        nc.vector.tensor_copy(key_w[:].rearrange("p (t m) -> p m t", t=PACK), dk_w[:].rearrange("p (m t) -> p m t", t=PACK))
         nc.vector.tensor_copy(x2_sc[:], x_sc[:].indirect(two_t[:]))
+        nc.vector.tensor_copy(key_w[:].rearrange("p (t m) -> p m t", t=PACK), dk_w[:].rearrange("p (m t) -> p m t", t=PACK))
         nc.vector.tensor_copy(xq_w[:], x_w[:].indirect(offs_t[:]))
 
-        g = pool.tile([P, PACK], F32, name="g", tag="dk_sc", align_bytes=64)
-        nc.sync.dma_start(g[:], gn.rearrange("(p t) o -> p (t o)", t=PACK))
-        HALF = N // 2
-        raws = {}
-        after = {("w2", 0): "d_w", ("w1", 0): "dk_w", ("w2", 1): "x_sc", ("w1", 1): "d_sc"}
-        for hf in range(2):
-            for name, w in (("w2", w2), ("w1", w1)):
-                raw = pool.tile([P, PACK, HALF], F32, name="raw_%s_%d" % (name, hf), tag=after[(name, hf)], align_bytes=64)
-                nc.sync.dma_start(raw[:], w.rearrange("(p j) n -> p j n", j=PACK)[:, :, hf * HALF:(hf + 1) * HALF])
-                raws[(name, hf)] = raw
+        w_bf, w_q, w_sc = {}, {}, {}
+
+        def cast_w(name, c0, c1, copy, grouped):
+            dst = grouped[:].rearrange("p (c i t) -> p c t i", i=4, t=PACK)
+            src = raws[(name, c0 // HALF)][:, :, c0 % HALF:c0 % HALF + c1 - c0].rearrange("p t (c i) -> p c t i", i=4)
+            copy(dst, src)
+            w_bf[(name, c0)] = grouped
+
+        def quant_w(name, c0, c1, codes):
+            scales = pool.tile([P, c1 - c0], U8, name="sc_%s_%d" % (name, c0), align_bytes=64)
+            nc.vector.quantize_mx(out=codes[:].bitcast(FP8X4), scales=scales[:], in_=w_bf[(name, c0)][:])
+            for m in range(c0 // P, c1 // P):
+                cols = slice(m * P - c0, (m + 1) * P - c0)
+                w_q[(name, m)] = codes[:, cols].bitcast(FP8X4)
+                w_sc[(name, m)] = scales[:, cols]
+
+        def tagged(shape, dtype, name, tag):
+            return pool.tile(shape, dtype, name=name, tag=tag, align_bytes=64)
 
         s_ps = [psum.tile([P, S], F32, name="s_ps%d" % t) for t in range(PACK)]
         for t in (3, 2, 1, 0):
@@ -99,78 +123,60 @@ def tile_picked_kmixunderghopm_none_p_kernel(tc, x_words, x_scales, d_words, d_s
             nc.tensor.matmul_mx(out=s_ps[t][:], lhsT=key_w[:, cols].bitcast(FP8X4), lhsT_scale=key_sc[:, cols],
                                 rhs=xq_w[:].bitcast(FP8X4), rhs_scale=xq_sc[:], start=True, stop=True)
         nc.scalar.activation(s[:, 3 * S:4 * S], s_ps[3][:], COPY, scale=0.0625)
-        nc.vector.tensor_scalar(s[:, 2 * S:3 * S], s_ps[2][:], 0.0625, None, ALU.mult)
-        nc.vector.tensor_copy(x2_w[:], x_w[:].indirect(two_t[:]))
-        for t in (1, 0):
+        for t in (2, 1, 0):
             nc.vector.tensor_scalar(s[:, t * S:(t + 1) * S], s_ps[t][:], 0.0625, None, ALU.mult)
+        nc.vector.tensor_copy(x2_w[:], x_w[:].indirect(two_t[:]))
         s3 = s[:, :PACK * S].rearrange("p (t j) -> p t j", t=PACK)
 
-        w_bf, w_q, w_sc = {}, {}, {}
-
-        def cast_w(name, m, copy, tag=None):
-            key = (name, m)
-            grouped = pool.tile([P, P * PACK], BF16, name="bf_%s_%d" % key, tag=tag or "bf_%s_%d" % key, align_bytes=64)
-            dst = grouped[:].rearrange("p (c i t) -> p c t i", i=4, t=PACK)
-            src = raws[(name, m // 2)][:, :, (m % 2) * P:(m % 2 + 1) * P].rearrange("p t (c i) -> p c t i", i=4)
-            copy(dst, src)
-            w_bf[key] = grouped
-
-        def quant_w(name, m):
-            key = (name, m)
-            w_q[key] = pool.tile([P, P], U32, name="q_%s_%d" % key, align_bytes=64)
-            w_sc[key] = pool.tile([P, P], U8, name="sc_%s_%d" % key, align_bytes=64)
-            nc.vector.quantize_mx(out=w_q[key][:].bitcast(FP8X4), scales=w_sc[key][:], in_=w_bf[key][:])
-
-        z_bf = pool.tile([P, S * PACK], BF16, name="z_bf", align_bytes=64)
+        z_bf = turn.tile([P, S * PACK], BF16, name="z_bf", offset=1536, align_bytes=64)
         z_q = pool.tile([P, S], U32, name="z_q", align_bytes=64)
         z_sc = pool.tile([P, S], U8, name="z_sc", align_bytes=64)
 
-        tiles = {}
-        for c0, c1 in ((0, 192), (192, 256)):
-            for nm in ("a", "b", "low", "dif"):
-                tiles[(nm, c0)] = pool.tile([P, PACK, c1 - c0], F32, name="%s%d" % (nm, c0), tag="%s%d" % (nm, c0), align_bytes=64)
-
-        def fetch(c0, c1, t0, t1):
-            a, b, low, dif = (tiles[(nm, c0)] for nm in ("a", "b", "low", "dif"))
+        def fetch(c0, c1, t0, t1, a, b, low, dif):
             for t in range(t1 - 1, t0 - 1, -1):
                 win = s[:, t * S:t * S + S_WIN]
                 nc.scalar.activation(a[:, t, :], win.indirect(n1_t[:, c0 // 16:c1 // 16]), COPY)
                 nc.scalar.activation(b[:, t, :], win.indirect(n2_t[:, c0 // 16:c1 // 16]), COPY)
-            nc.vector.tensor_tensor(low[:, t0:t1, :], a[:, t0:t1, :], b[:, t0:t1, :], ALU.min)
-            nc.vector.tensor_tensor(dif[:, t0:t1, :], s3[:, t0:t1, c0:c1], low[:, t0:t1, :], ALU.subtract)
+            nc.vector.tensor_tensor(low, a[:, t0:t1, :], b[:, t0:t1, :], ALU.min)
+            nc.vector.tensor_tensor(dif[:, t0:t1, :], s3[:, t0:t1, c0:c1], low, ALU.subtract)
 
-        def gain(c0, c1):
+        def gain(c0, c1, dif):
             nc.vector.tensor_tensor(
                 z_bf[:, c0 * PACK:c1 * PACK].rearrange("p (c i t) -> p c t i", i=4, t=PACK),
-                tiles[("dif", c0)][:].rearrange("p t (c i) -> p c t i", i=4),
+                dif[:].rearrange("p t (c i) -> p c t i", i=4),
                 g[:].unsqueeze(1).unsqueeze(3).to_broadcast([P, (c1 - c0) // 4, PACK, 4]), ALU.mult)
 
         def quant_z(c0, c1):
             nc.vector.quantize_mx(out=z_q[:, c0:c1].bitcast(FP8X4), scales=z_sc[:, c0:c1], in_=z_bf[:, c0 * PACK:c1 * PACK])
 
-        cast_w("w2", 0, nc.vector.tensor_copy)
-        fetch(0, 192, 2, 4)
-        quant_w("w2", 0)
-        cast_w("w1", 0, nc.vector.tensor_copy)
-        fetch(0, 192, 1, 2)
-        quant_w("w1", 0)
-        fetch(0, 192, 0, 1)
-        gain(0, 192)
-        fetch(192, 256, 1, 4)
-        quant_z(0, 128)
-        quant_z(128, 192)
-        fetch(192, 256, 0, 1)
-        gain(192, 256)
-        quant_z(192, 256)
-        cast_w("w2", 1, nc.scalar.copy, "a0")
-        cast_w("w1", 1, nc.scalar.copy, "b0")
+        CUT = 128
+        a0, b0, dif0 = (tagged([P, PACK, CUT], F32, nm, nm) for nm in ("a0", "b0", "dif0"))
+        fetch(0, CUT, 2, 4, a0, b0, tagged([P, 2, CUT], F32, "low_hi", "low_hi")[:], dif0)
+        fetch(0, CUT, 0, 2, a0, b0, tagged([P, 2, CUT], F32, "low_lo", "low_lo")[:], dif0)
+        gain(0, CUT, dif0)
+        quant_z(0, CUT)
+        ab1 = tagged([P, 2 * PACK, S - CUT], F32, "ab1", "x_w")
+        a1, b1 = ab1[:, :PACK, :], ab1[:, PACK:, :]
+        dif1 = tagged([P, PACK, S - CUT], F32, "dif1", "dif1")
+        low1 = tagged([P, PACK, S - CUT], F32, "low1", "dif0")
+        fetch(CUT, S, 2, 4, a1, b1, low1[:, 2:4, :], dif1)
+        fetch(CUT, S, 1, 2, a1, b1, low1[:, 1:2, :], dif1)
+        fetch(CUT, S, 0, 1, a1, b1, low1[:, 0:1, :], dif1)
+        cast_w("w2", 0, P, nc.scalar.copy, tagged([P, P * PACK], BF16, "bf_w2_0", "a0"))
+        cast_w("w1", 0, P, nc.scalar.copy, tagged([P, P * PACK], BF16, "bf_w1_0", "b0"))
+        cast_w("w2", P, 2 * P, nc.scalar.copy, tagged([P, P * PACK], BF16, "bf_w2_1", "low_hi"))
+        cast_w("w1", P, 2 * P, nc.scalar.copy, tagged([P, P * PACK], BF16, "bf_w1_1", "low_lo"))
+        gain(CUT, S, dif1)
+        quant_w("w2", 0, P, tagged([P, P], U32, "q_w2_0", "dif0"))
+        quant_z(CUT, S)
+        quant_w("w1", 0, P, tagged([P, P], U32, "q_w1_0", "dif1"))
 
         h_ps = [psum.tile([P, S], F32, name="h_ps%d" % m) for m in range(4)]
 
         def product(m, copy):
-            nc.tensor.matmul_mx(out=h_ps[m][:], lhsT=w_q[("w2", m)][:].bitcast(FP8X4), lhsT_scale=w_sc[("w2", m)][:],
+            nc.tensor.matmul_mx(out=h_ps[m][:], lhsT=w_q[("w2", m)], lhsT_scale=w_sc[("w2", m)],
                                 rhs=x2_w[:].bitcast(FP8X4), rhs_scale=x2_sc[:], start=True, stop=False)
-            nc.tensor.matmul_mx(out=h_ps[m][:], lhsT=w_q[("w1", m)][:].bitcast(FP8X4), lhsT_scale=w_sc[("w1", m)][:],
+            nc.tensor.matmul_mx(out=h_ps[m][:], lhsT=w_q[("w1", m)], lhsT_scale=w_sc[("w1", m)],
                                 rhs=z_q[:].bitcast(FP8X4), rhs_scale=z_sc[:], start=False, stop=True)
             copy(h[m][:, :S], h_ps[m][:])
 
@@ -190,26 +196,23 @@ def tile_picked_kmixunderghopm_none_p_kernel(tc, x_words, x_scales, d_words, d_s
                 nc.vector.tensor_tensor(res[:], st[m][:, c0:c1], far[:], ALU.max)
                 nc.sync.dma_start(out[m * P:(m + 1) * P, c0:c1], res[:])
 
-        def weights(m):
-            cast_w("w2", m, nc.vector.tensor_copy)
-            cast_w("w1", m, nc.vector.tensor_copy)
-            quant_w("w2", m)
-            quant_w("w1", m)
-
         whole = [(0, S)]
         product(0, nc.scalar.copy)
-        quant_w("w2", 1)
-        quant_w("w1", 1)
+        cast_w("w2", 2 * P, 3 * P, nc.vector.tensor_copy, turn.tile([P, P * PACK], BF16, name="bf_w2_2", offset=1024, align_bytes=64))
+        cast_w("w1", 2 * P, 3 * P, nc.vector.tensor_copy, turn.tile([P, P * PACK], BF16, name="bf_w1_2", offset=3072, align_bytes=64))
+        quant_w("w2", P, 2 * P, turn.tile([P, P], U32, name="q_w2_1", offset=2048, align_bytes=64))
+        quant_w("w1", P, 2 * P, turn.tile([P, P], U32, name="q_w1_1", offset=2560, align_bytes=64))
         product(1, nc.vector.tensor_copy)
-        weights(2)
-        members(0, whole)
+        quant_w("w2", 2 * P, 3 * P, tagged([P, P], U32, "q_w2_2", "q_w2_2"))
+        quant_w("w1", 2 * P, 3 * P, tagged([P, P], U32, "q_w1_2", "q_w1_2"))
         product(2, nc.vector.tensor_copy)
-        weights(3)
-        members(1, whole)
+        cast_w("w2", 3 * P, N, nc.vector.tensor_copy, tagged([P, P * PACK], BF16, "bf_w2_3", "low_hi"))
+        cast_w("w1", 3 * P, N, nc.vector.tensor_copy, tagged([P, P * PACK], BF16, "bf_w1_3", "low_lo"))
+        quant_w("w2", 3 * P, N, tagged([P, P], U32, "q_w2_3", "q_w2_3"))
+        quant_w("w1", 3 * P, N, tagged([P, P], U32, "q_w1_3", "q_w1_3"))
         product(3, nc.vector.tensor_copy)
-        finish(0, whole)
-        members(2, whole)
-        finish(1, whole)
-        members(3, [(0, 192), (192, 256)])
-        finish(2, whole)
-        finish(3, [(0, 192), (192, 256)])
+        for m in range(4):
+            members(m, whole)
+        for m in range(3):
+            finish(m, whole)
+        finish(3, [(0, 192), (192, S)])

@@ -39,25 +39,25 @@ def tile_picked_kmixunderghopm_none_p_kernel(tc, x_words, x_scales, d_words, d_s
         x_sc = pool.tile([P, T], U8, name="x_sc", align_bytes=64)
         nc.vector.memset(d_sc[:, :T // 2].bitcast(I32), 0)
         nc.gpsimd.memset(d_sc[:, T // 2:].bitcast(I32), 0)
-        nc.vector.memset(x_sc[:, :T // 2].bitcast(I32), 0)
-        nc.gpsimd.memset(x_sc[:, T // 2:].bitcast(I32), 0)
-        S_WIN, H_WIN, ST_WIN = 384, J + 16, S + 16
-        s = pool.tile([P, (PACK - 1) * S + S_WIN], F32, name="s")
+        nc.vector.memset(x_sc[:].bitcast(I32), 0)
+        H_WIN, ST_WIN = J + 16, S + 16
+        s = [pool.tile([P, ST_WIN], F32, name="s%d" % t) for t in range(PACK)]
         h = [pool.tile([P, H_WIN], F32, name="h%d" % m) for m in range(4)]
         st = [pool.tile([P, ST_WIN], F32, name="st%d" % m) for m in range(4)]
-        nc.vector.memset(s[:, PACK * S:], 0.0)
         for m in range(4):
+            nc.vector.memset(s[m][:, S:], 0.0)
             nc.vector.memset(h[m][:, S:], 0.0)
             nc.vector.memset(st[m][:, S:], 0.0)
 
         k1_t = load_list(k1, "k1")
         offs_t = load_list(offs, "offs")
-        nc.sync.dma_start(d_sc[0:P:8, :].bitcast(I32), d_scales[0].bitcast(I32))
-        for a in range(4):
-            nc.sync.dma_start(x_sc[a:P:32, :].bitcast(I32), x_scales[0, a:16:4, :].bitcast(I32))
+        n1_t = load_list(n1, "n1")
+        for e in range(2):
+            nc.sync.dma_start(d_sc[e:P:16, :].bitcast(I32), d_scales[0, e:16:2, :].bitcast(I32))
         d_w = pool.tile([P, T], U32, name="d_w", align_bytes=64)
         nc.sync.dma_start(d_w[:].bitcast(I32), d_words[0].rearrange("p n t -> p (n t)").bitcast(I32))
-        two_t = load_list(two, "two")
+        for a in range(4):
+            nc.sync.dma_start(x_sc[a:P:32, :].bitcast(I32), x_scales[0, a:16:4, :].bitcast(I32))
         HALF = N // 2
         raws = {}
 
@@ -66,19 +66,19 @@ def tile_picked_kmixunderghopm_none_p_kernel(tc, x_words, x_scales, d_words, d_s
             nc.sync.dma_start(raw[:], w.rearrange("(p j) n -> p j n", j=PACK)[:, :, hf * HALF:(hf + 1) * HALF])
             raws[(name, hf)] = raw
 
-        x_w = pool.tile([P, T], U32, name="x_w", tag="x_w", align_bytes=64)
+        x_w = pool.tile([P, T], U32, name="x_w", align_bytes=64)
         nc.sync.dma_start(x_w[:].bitcast(I32), x_words[0].rearrange("p n t -> p (n t)").bitcast(I32))
         g = pool.tile([P, PACK], F32, name="g")
         nc.sync.dma_start(g[:], gn.rearrange("(p t) o -> p (t o)", t=PACK))
-        n1_t = load_list(n1, "n1")
         n2_t = load_list(n2, "n2")
 
         dk_sc = pool.tile([P, H], U8, name="dk_sc", align_bytes=64)
         nc.vector.tensor_copy(dk_sc[:], d_sc[:].indirect(k1_t[:]))
         key_sc = pool.tile([P, H], U8, name="key_sc", align_bytes=64)
         nc.vector.tensor_copy(key_sc[:].rearrange("p (t m) -> p m t", t=PACK), dk_sc[:].rearrange("p (m t) -> p m t", t=PACK))
-        for a in range(1, 4):
-            nc.sync.dma_start(key_sc[a:P:32, :].bitcast(I32), key_sc[8 * a:P:32, :].bitcast(I32))
+        nc.sync.dma_start(key_sc[2:P:32, :].bitcast(I32), key_sc[16:P:32, :].bitcast(I32))
+        two_t = load_list(two, "two")
+        nc.sync.dma_start(key_sc[3:P:32, :].bitcast(I32), key_sc[17:P:32, :].bitcast(I32))
         load_weights("w2", w2, 0)
         load_weights("w1", w1, 0)
         load_weights("w2", w2, 1)
@@ -92,10 +92,9 @@ def tile_picked_kmixunderghopm_none_p_kernel(tc, x_words, x_scales, d_words, d_s
         key_w = pool.tile([P, H], U32, name="key_w", align_bytes=64)
         xq_w = pool.tile([P, S], U32, name="xq_w", align_bytes=64)
         x2_w = pool.tile([P, S], U32, name="x2_w", align_bytes=64)
-        nc.vector.tensor_copy(xq_sc[:], x_sc[:].indirect(offs_t[:]))
         nc.vector.tensor_copy(dk_w[:], d_w[:].indirect(k1_t[:]))
-        nc.vector.tensor_copy(x2_sc[:], x_sc[:].indirect(two_t[:]))
         nc.vector.tensor_copy(key_w[:].rearrange("p (t m) -> p m t", t=PACK), dk_w[:].rearrange("p (m t) -> p m t", t=PACK))
+        nc.vector.tensor_copy(xq_sc[:], x_sc[:].indirect(offs_t[:]))
         nc.vector.tensor_copy(xq_w[:], x_w[:].indirect(offs_t[:]))
 
         w_bf, w_q, w_sc = {}, {}, {}
@@ -118,58 +117,52 @@ def tile_picked_kmixunderghopm_none_p_kernel(tc, x_words, x_scales, d_words, d_s
             return pool.tile(shape, dtype, name=name, tag=tag, align_bytes=64)
 
         s_ps = [psum.tile([P, S], F32, name="s_ps%d" % t) for t in range(PACK)]
-        for t in (3, 2, 1, 0):
+        for t in range(PACK):
             cols = slice(t * P, (t + 1) * P)
             nc.tensor.matmul_mx(out=s_ps[t][:], lhsT=key_w[:, cols].bitcast(FP8X4), lhsT_scale=key_sc[:, cols],
                                 rhs=xq_w[:].bitcast(FP8X4), rhs_scale=xq_sc[:], start=True, stop=True)
-        nc.scalar.activation(s[:, 3 * S:4 * S], s_ps[3][:], COPY, scale=0.0625)
-        for t in (2, 1, 0):
-            nc.vector.tensor_scalar(s[:, t * S:(t + 1) * S], s_ps[t][:], 0.0625, None, ALU.mult)
+        neg_g = pool.tile([P, PACK], F32, name="neg_g")
+        nc.vector.tensor_scalar(neg_g[:], g[:], -1.0, None, ALU.mult)
+        nc.scalar.activation(s[0][:, :S], s_ps[0][:], COPY, scale=0.0625)
+        nc.vector.tensor_copy(x2_sc[:], x_sc[:].indirect(two_t[:]))
+        for t in range(1, PACK):
+            nc.vector.tensor_scalar(s[t][:, :S], s_ps[t][:], 0.0625, None, ALU.mult)
         nc.vector.tensor_copy(x2_w[:], x_w[:].indirect(two_t[:]))
-        s3 = s[:, :PACK * S].rearrange("p (t j) -> p t j", t=PACK)
 
+        z32 = tagged([P, PACK, S], F32, "z32", "z32")
         z_bf = turn.tile([P, S * PACK], BF16, name="z_bf", offset=1536, align_bytes=64)
         z_q = pool.tile([P, S], U32, name="z_q", align_bytes=64)
         z_sc = pool.tile([P, S], U8, name="z_sc", align_bytes=64)
+        gs = tagged([P, PACK, S], F32, "gs", "gs")
 
-        def fetch(c0, c1, t0, t1, a, b, low, dif):
-            for t in range(t1 - 1, t0 - 1, -1):
-                win = s[:, t * S:t * S + S_WIN]
-                nc.scalar.activation(a[:, t, :], win.indirect(n1_t[:, c0 // 16:c1 // 16]), COPY)
-                nc.scalar.activation(b[:, t, :], win.indirect(n2_t[:, c0 // 16:c1 // 16]), COPY)
-            nc.vector.tensor_tensor(low, a[:, t0:t1, :], b[:, t0:t1, :], ALU.min)
-            nc.vector.tensor_tensor(dif[:, t0:t1, :], s3[:, t0:t1, c0:c1], low, ALU.subtract)
+        def fetch(t, c0, c1):
+            a = tagged([P, c1 - c0], F32, "a%d_%d" % (t, c0), "a%d_%d" % (t, c0))
+            b = tagged([P, c1 - c0], F32, "b%d_%d" % (t, c0), "b%d_%d" % (t, c0))
+            low = tagged([P, c1 - c0], F32, "low%d_%d" % (t, c0), "low%d_%d" % (t, c0))
+            nc.scalar.activation(a[:], s[t][:].indirect(n1_t[:, c0 // 16:c1 // 16]), COPY)
+            nc.scalar.activation(b[:], s[t][:].indirect(n2_t[:, c0 // 16:c1 // 16]), COPY)
+            nc.vector.tensor_tensor(low[:], a[:], b[:], ALU.min)
+            nc.vector.scalar_tensor_tensor(z32[:, t, c0:c1], low[:], neg_g[:, t:t + 1], gs[:, t, c0:c1], ALU.mult, ALU.add)
 
-        def gain(c0, c1, dif):
-            nc.vector.tensor_tensor(
-                z_bf[:, c0 * PACK:c1 * PACK].rearrange("p (c i t) -> p c t i", i=4, t=PACK),
-                dif[:].rearrange("p t (c i) -> p c t i", i=4),
-                g[:].unsqueeze(1).unsqueeze(3).to_broadcast([P, (c1 - c0) // 4, PACK, 4]), ALU.mult)
+        def round_z(c0, c1):
+            nc.vector.tensor_copy(z_bf[:, c0 * PACK:c1 * PACK].rearrange("p (c i t) -> p c t i", i=4, t=PACK),
+                                  z32[:, :, c0:c1].rearrange("p t (c i) -> p c t i", i=4))
 
         def quant_z(c0, c1):
             nc.vector.quantize_mx(out=z_q[:, c0:c1].bitcast(FP8X4), scales=z_sc[:, c0:c1], in_=z_bf[:, c0 * PACK:c1 * PACK])
 
-        CUT = 128
-        a0, b0, dif0 = (tagged([P, PACK, CUT], F32, nm, nm) for nm in ("a0", "b0", "dif0"))
-        fetch(0, CUT, 2, 4, a0, b0, tagged([P, 2, CUT], F32, "low_hi", "low_hi")[:], dif0)
-        fetch(0, CUT, 0, 2, a0, b0, tagged([P, 2, CUT], F32, "low_lo", "low_lo")[:], dif0)
-        gain(0, CUT, dif0)
-        quant_z(0, CUT)
-        ab1 = tagged([P, 2 * PACK, S - CUT], F32, "ab1", "x_w")
-        a1, b1 = ab1[:, :PACK, :], ab1[:, PACK:, :]
-        dif1 = tagged([P, PACK, S - CUT], F32, "dif1", "dif1")
-        low1 = tagged([P, PACK, S - CUT], F32, "low1", "dif0")
-        fetch(CUT, S, 2, 4, a1, b1, low1[:, 2:4, :], dif1)
-        fetch(CUT, S, 1, 2, a1, b1, low1[:, 1:2, :], dif1)
-        fetch(CUT, S, 0, 1, a1, b1, low1[:, 0:1, :], dif1)
-        cast_w("w2", 0, P, nc.scalar.copy, tagged([P, P * PACK], BF16, "bf_w2_0", "a0"))
-        cast_w("w1", 0, P, nc.scalar.copy, tagged([P, P * PACK], BF16, "bf_w1_0", "b0"))
-        cast_w("w2", P, 2 * P, nc.scalar.copy, tagged([P, P * PACK], BF16, "bf_w2_1", "low_hi"))
-        cast_w("w1", P, 2 * P, nc.scalar.copy, tagged([P, P * PACK], BF16, "bf_w1_1", "low_lo"))
-        gain(CUT, S, dif1)
-        quant_w("w2", 0, P, tagged([P, P], U32, "q_w2_0", "dif0"))
-        quant_z(CUT, S)
-        quant_w("w1", 0, P, tagged([P, P], U32, "q_w1_0", "dif1"))
+        for t in range(PACK):
+            nc.vector.tensor_scalar(gs[:, t, :], s[t][:, :S], g[:, t:t + 1], None, ALU.mult)
+        for t in range(PACK):
+            fetch(t, 0, S)
+        cast_w("w2", 0, P, nc.scalar.copy, tagged([P, P * PACK], BF16, "bf_w2_0", "a0_0"))
+        cast_w("w1", 0, P, nc.scalar.copy, tagged([P, P * PACK], BF16, "bf_w1_0", "b0_0"))
+        cast_w("w2", P, 2 * P, nc.scalar.copy, tagged([P, P * PACK], BF16, "bf_w2_1", "b3_0"))
+        cast_w("w1", P, 2 * P, nc.scalar.copy, tagged([P, P * PACK], BF16, "bf_w1_1", "gs"))
+        round_z(0, S)
+        quant_w("w2", 0, P, tagged([P, P], U32, "q_w2_0", "low3_0"))
+        quant_z(0, S)
+        quant_w("w1", 0, P, tagged([P, P], U32, "q_w1_0", "z32"))
 
         h_ps = [psum.tile([P, S], F32, name="h_ps%d" % m) for m in range(4)]
 
@@ -206,8 +199,8 @@ def tile_picked_kmixunderghopm_none_p_kernel(tc, x_words, x_scales, d_words, d_s
         quant_w("w2", 2 * P, 3 * P, tagged([P, P], U32, "q_w2_2", "q_w2_2"))
         quant_w("w1", 2 * P, 3 * P, tagged([P, P], U32, "q_w1_2", "q_w1_2"))
         product(2, nc.vector.tensor_copy)
-        cast_w("w2", 3 * P, N, nc.vector.tensor_copy, tagged([P, P * PACK], BF16, "bf_w2_3", "low_hi"))
-        cast_w("w1", 3 * P, N, nc.vector.tensor_copy, tagged([P, P * PACK], BF16, "bf_w1_3", "low_lo"))
+        cast_w("w2", 3 * P, N, nc.vector.tensor_copy, tagged([P, P * PACK], BF16, "bf_w2_3", "b3_0"))
+        cast_w("w1", 3 * P, N, nc.vector.tensor_copy, tagged([P, P * PACK], BF16, "bf_w1_3", "gs"))
         quant_w("w2", 3 * P, N, tagged([P, P], U32, "q_w2_3", "q_w2_3"))
         quant_w("w1", 3 * P, N, tagged([P, P], U32, "q_w1_3", "q_w1_3"))
         product(3, nc.vector.tensor_copy)

@@ -19,15 +19,23 @@ S = 256
 H = 512
 N = 512
 J = 512
-FLOPS = 3 * 2 * 512 * 512 * 256
+TILES = N // P
+W_HALF = N // 2
+S_HALF = S // 2
+LAST_CUT = 192
+SPARE = 16
+SCORE_FACTOR = 0.0625
+FLOPS = 3 * 2 * 512 * 512 * S
 
 
-def tile_picked_kmixunderghopm_none_p_kernel(tc, x_words, x_scales, d_words, d_scales, gn, w1, w2, offs, k1, n1, n2, two, n3, n4, out):
+def tile_picked_kmixunderghopm_none_p_kernel(
+    tc, x_words, x_scales, d_words, d_scales, gn, w1, w2, offs, k1, n1, n2, two, n3, n4, out
+):
     nc = tc.nc
     with ExitStack() as ctx:
         lists = ctx.enter_context(tc.tile_pool(name="lists", bufs=1))
         pool = ctx.enter_context(tc.tile_pool(name="pool", bufs=1))
-        turn = ctx.enter_context(tc.tile_pool(name="turn", bufs=1))
+        after_z = ctx.enter_context(tc.tile_pool(name="after_z", bufs=1))
         psum = ctx.enter_context(tc.psum_pool(name="psum", bufs=1))
 
         def load_list(src, name):
@@ -35,177 +43,201 @@ def tile_picked_kmixunderghopm_none_p_kernel(tc, x_words, x_scales, d_words, d_s
             nc.sync.dma_start(tile[:], src)
             return tile
 
+        def buffer(shape, dtype, name, tag):
+            return pool.tile(shape, dtype, name=name, tag=tag, align_bytes=64)
+
         d_sc = pool.tile([P, T], U8, name="d_sc", align_bytes=64)
         x_sc = pool.tile([P, T], U8, name="x_sc", align_bytes=64)
         nc.vector.memset(d_sc[:, :T // 2].bitcast(I32), 0)
         nc.gpsimd.memset(d_sc[:, T // 2:].bitcast(I32), 0)
         nc.vector.memset(x_sc[:].bitcast(I32), 0)
-        H_WIN, ST_WIN = J + 16, S + 16
-        s = [pool.tile([P, ST_WIN], F32, name="s%d" % t) for t in range(PACK)]
-        h = [pool.tile([P, H_WIN], F32, name="h%d" % m) for m in range(4)]
-        st = [pool.tile([P, ST_WIN], F32, name="st%d" % m) for m in range(4)]
-        for m in range(4):
-            nc.vector.memset(s[m][:, S:], 0.0)
-            nc.vector.memset(h[m][:, S:], 0.0)
-            nc.vector.memset(st[m][:, S:], 0.0)
+
+        s = [pool.tile([P, S + SPARE], F32, name="s%d" % t) for t in range(PACK)]
+        h = [pool.tile([P, J + SPARE], F32, name="h%d" % m) for m in range(TILES)]
+        st = [pool.tile([P, S + SPARE], F32, name="st%d" % m) for m in range(TILES)]
+        for windows in zip(s, h, st):
+            for window in windows:
+                nc.vector.memset(window[:, S:], 0.0)
 
         k1_t = load_list(k1, "k1")
         offs_t = load_list(offs, "offs")
         n1_t = load_list(n1, "n1")
         for e in range(2):
             nc.sync.dma_start(d_sc[e:P:16, :].bitcast(I32), d_scales[0, e:16:2, :].bitcast(I32))
-        d_w = pool.tile([P, T], U32, name="d_w", align_bytes=64)
+        d_w = buffer([P, T], U32, "d_w", "d_w")
         nc.sync.dma_start(d_w[:].bitcast(I32), d_words[0].rearrange("p n t -> p (n t)").bitcast(I32))
         for a in range(4):
             nc.sync.dma_start(x_sc[a:P:32, :].bitcast(I32), x_scales[0, a:16:4, :].bitcast(I32))
-        HALF = N // 2
-        raws = {}
-
-        def load_weights(name, w, hf):
-            raw = pool.tile([P, PACK, HALF], F32, name="raw_%s_%d" % (name, hf))
-            nc.sync.dma_start(raw[:], w.rearrange("(p j) n -> p j n", j=PACK)[:, :, hf * HALF:(hf + 1) * HALF])
-            raws[(name, hf)] = raw
-
-        x_w = pool.tile([P, T], U32, name="x_w", align_bytes=64)
+        x_w = buffer([P, T], U32, "x_w", "x_w")
         nc.sync.dma_start(x_w[:].bitcast(I32), x_words[0].rearrange("p n t -> p (n t)").bitcast(I32))
-        g = pool.tile([P, PACK], F32, name="g")
-        nc.sync.dma_start(g[:], gn.rearrange("(p t) o -> p (t o)", t=PACK))
+        gain = pool.tile([P, PACK], F32, name="gain")
+        nc.sync.dma_start(gain[:], gn.rearrange("(p t) o -> p (t o)", t=PACK))
         n2_t = load_list(n2, "n2")
 
-        dk_sc = pool.tile([P, H], U8, name="dk_sc", align_bytes=64)
+        dk_sc = buffer([P, H], U8, "dk_sc", "dk_sc")
         nc.vector.tensor_copy(dk_sc[:], d_sc[:].indirect(k1_t[:]))
-        key_sc = pool.tile([P, H], U8, name="key_sc", align_bytes=64)
-        nc.vector.tensor_copy(key_sc[:].rearrange("p (t m) -> p m t", t=PACK), dk_sc[:].rearrange("p (m t) -> p m t", t=PACK))
+        key_sc = buffer([P, H], U8, "key_sc", "key_sc")
+        nc.vector.tensor_copy(
+            key_sc[:].rearrange("p (t m) -> p m t", t=PACK), dk_sc[:].rearrange("p (m t) -> p m t", t=PACK)
+        )
         nc.sync.dma_start(key_sc[2:P:32, :].bitcast(I32), key_sc[16:P:32, :].bitcast(I32))
         two_t = load_list(two, "two")
         nc.sync.dma_start(key_sc[3:P:32, :].bitcast(I32), key_sc[17:P:32, :].bitcast(I32))
-        load_weights("w2", w2, 0)
-        load_weights("w1", w1, 0)
-        load_weights("w2", w2, 1)
-        load_weights("w1", w1, 1)
+
+        w_raw = {}
+        for half in range(2):
+            for name, w in (("w2", w2), ("w1", w1)):
+                raw = pool.tile([P, PACK, W_HALF], F32, name="raw_%s_%d" % (name, half))
+                rows = w.rearrange("(p j) n -> p j n", j=PACK)
+                nc.sync.dma_start(raw[:], rows[:, :, half * W_HALF:(half + 1) * W_HALF])
+                w_raw[(name, half)] = raw
         n3_t = load_list(n3, "n3")
         n4_t = load_list(n4, "n4")
 
-        xq_sc = pool.tile([P, S], U8, name="xq_sc", align_bytes=64)
-        x2_sc = pool.tile([P, S], U8, name="x2_sc", align_bytes=64)
-        dk_w = pool.tile([P, H], U32, name="dk_w", align_bytes=64)
-        key_w = pool.tile([P, H], U32, name="key_w", align_bytes=64)
-        xq_w = pool.tile([P, S], U32, name="xq_w", align_bytes=64)
-        x2_w = pool.tile([P, S], U32, name="x2_w", align_bytes=64)
+        xq_sc = buffer([P, S], U8, "xq_sc", "xq_sc")
+        x2_sc = buffer([P, S], U8, "x2_sc", "x2_sc")
+        dk_w = buffer([P, H], U32, "dk_w", "dk_w")
+        key_w = buffer([P, H], U32, "key_w", "key_w")
+        xq_w = buffer([P, S], U32, "xq_w", "xq_w")
+        x2_w = buffer([P, S], U32, "x2_w", "x2_w")
         nc.vector.tensor_copy(dk_w[:], d_w[:].indirect(k1_t[:]))
-        nc.vector.tensor_copy(key_w[:].rearrange("p (t m) -> p m t", t=PACK), dk_w[:].rearrange("p (m t) -> p m t", t=PACK))
+        nc.vector.tensor_copy(
+            key_w[:].rearrange("p (t m) -> p m t", t=PACK), dk_w[:].rearrange("p (m t) -> p m t", t=PACK)
+        )
         nc.vector.tensor_copy(xq_sc[:], x_sc[:].indirect(offs_t[:]))
         nc.vector.tensor_copy(xq_w[:], x_w[:].indirect(offs_t[:]))
 
-        w_bf, w_q, w_sc = {}, {}, {}
-
-        def cast_w(name, c0, c1, copy, grouped):
-            dst = grouped[:].rearrange("p (c i t) -> p c t i", i=4, t=PACK)
-            src = raws[(name, c0 // HALF)][:, :, c0 % HALF:c0 % HALF + c1 - c0].rearrange("p t (c i) -> p c t i", i=4)
-            copy(dst, src)
-            w_bf[(name, c0)] = grouped
-
-        def quant_w(name, c0, c1, codes):
-            scales = pool.tile([P, c1 - c0], U8, name="sc_%s_%d" % (name, c0), align_bytes=64)
-            nc.vector.quantize_mx(out=codes[:].bitcast(FP8X4), scales=scales[:], in_=w_bf[(name, c0)][:])
-            for m in range(c0 // P, c1 // P):
-                cols = slice(m * P - c0, (m + 1) * P - c0)
-                w_q[(name, m)] = codes[:, cols].bitcast(FP8X4)
-                w_sc[(name, m)] = scales[:, cols]
-
-        def tagged(shape, dtype, name, tag):
-            return pool.tile(shape, dtype, name=name, tag=tag, align_bytes=64)
-
-        s_ps = [psum.tile([P, S], F32, name="s_ps%d" % t) for t in range(PACK)]
+        s_ps = [psum.tile([P, S], F32, name="s_ps%d" % t, tag="s_ps%d" % t) for t in range(PACK)]
         for t in range(PACK):
             cols = slice(t * P, (t + 1) * P)
-            nc.tensor.matmul_mx(out=s_ps[t][:], lhsT=key_w[:, cols].bitcast(FP8X4), lhsT_scale=key_sc[:, cols],
-                                rhs=xq_w[:].bitcast(FP8X4), rhs_scale=xq_sc[:], start=True, stop=True)
-        neg_g = pool.tile([P, PACK], F32, name="neg_g")
-        nc.vector.tensor_scalar(neg_g[:], g[:], -1.0, None, ALU.mult)
-        nc.scalar.activation(s[0][:, :S], s_ps[0][:], COPY, scale=0.0625)
+            nc.tensor.matmul_mx(
+                out=s_ps[t][:], lhsT=key_w[:, cols].bitcast(FP8X4), lhsT_scale=key_sc[:, cols],
+                rhs=xq_w[:].bitcast(FP8X4), rhs_scale=xq_sc[:], start=True, stop=True,
+            )
+        neg_gain = pool.tile([P, PACK], F32, name="neg_gain")
+        nc.vector.tensor_scalar(neg_gain[:], gain[:], -1.0, None, ALU.mult)
+        nc.scalar.activation(s[0][:, :S], s_ps[0][:], COPY, scale=SCORE_FACTOR)
         nc.vector.tensor_copy(x2_sc[:], x_sc[:].indirect(two_t[:]))
         for t in range(1, PACK):
-            nc.vector.tensor_scalar(s[t][:, :S], s_ps[t][:], 0.0625, None, ALU.mult)
+            nc.vector.tensor_scalar(s[t][:, :S], s_ps[t][:], SCORE_FACTOR, None, ALU.mult)
+
+        w_bf, w_q, w_sc = {}, {}, {}
+
+        def round_w(name, m, copy, grouped):
+            c0 = m * P % W_HALF
+            src = w_raw[(name, m * P // W_HALF)][:, :, c0:c0 + P]
+            copy(
+                grouped[:].rearrange("p (c i t) -> p c t i", i=4, t=PACK), src.rearrange("p t (c i) -> p c t i", i=4)
+            )
+            w_bf[(name, m)] = grouped
+
+        def quantise_w(name, m, codes):
+            scales = pool.tile([P, P], U8, name="sc_%s_%d" % (name, m), align_bytes=64)
+            nc.vector.quantize_mx(out=codes[:].bitcast(FP8X4), scales=scales[:], in_=w_bf[(name, m)][:])
+            w_q[(name, m)], w_sc[(name, m)] = codes, scales
+
+        bf_bytes, q_bytes = 2 * P * PACK, 4 * P
+        z_bf_at = bf_bytes + q_bytes
+        z32 = pool.tile([P, 2, PACK, S_HALF], F32, name="z32")
+        z_bf = after_z.tile([P, S * PACK], BF16, name="z_bf", offset=z_bf_at, align_bytes=64)
+        z_q = buffer([P, S], U32, "z_q", "z_q")
+        z_sc = buffer([P, S], U8, "z_sc", "z_sc")
+        gs = buffer([P, PACK, S], F32, "gs", "gs")
+
+        def gained_scores(t):
+            nc.vector.tensor_scalar(gs[:, t, :], s[t][:, :S], gain[:, t:t + 1], None, ALU.mult)
+
+        def make_z(t, c0, c1):
+            at_n1, at_n2, low = (
+                buffer([P, c1 - c0], F32, "%s%d_%d" % (role, t, c0), "%s%d_%d" % (role, t, c0))
+                for role in ("at_n1_", "at_n2_", "low_")
+            )
+            nc.scalar.activation(at_n1[:], s[t][:].indirect(n1_t[:, c0 // 16:c1 // 16]), COPY)
+            nc.scalar.activation(at_n2[:], s[t][:].indirect(n2_t[:, c0 // 16:c1 // 16]), COPY)
+            nc.vector.tensor_tensor(low[:], at_n1[:], at_n2[:], ALU.min)
+            nc.vector.scalar_tensor_tensor(
+                z32[:, c0 // S_HALF:c1 // S_HALF, t, :], low[:].rearrange("p (u j) -> p u j", j=S_HALF),
+                neg_gain[:, t:t + 1], gs[:, t, c0:c1].rearrange("p (u j) -> p u j", j=S_HALF), ALU.mult, ALU.add,
+            )
+
+        def round_z(half):
+            dst = z_bf[:, half * S_HALF * PACK:(half + 1) * S_HALF * PACK]
+            nc.vector.tensor_copy(
+                dst.rearrange("p (c i t) -> p c t i", i=4, t=PACK),
+                z32[:, half, :, :].rearrange("p t (c i) -> p c t i", i=4),
+            )
+
+        def quantise_z(half):
+            cols = slice(half * S_HALF, (half + 1) * S_HALF)
+            src = z_bf[:, half * S_HALF * PACK:(half + 1) * S_HALF * PACK]
+            nc.vector.quantize_mx(out=z_q[:, cols].bitcast(FP8X4), scales=z_sc[:, cols], in_=src)
+
+        gained_scores(0)
         nc.vector.tensor_copy(x2_w[:], x_w[:].indirect(two_t[:]))
+        make_z(0, 0, S)
+        gained_scores(1)
+        round_w("w2", 0, nc.vector.tensor_copy, buffer([P, P * PACK], BF16, "bf_w2_0", "bf_w2_0"))
+        make_z(1, 0, S)
+        gained_scores(2)
+        round_w("w1", 0, nc.vector.tensor_copy, buffer([P, P * PACK], BF16, "bf_w1_0", "bf_w1_0"))
+        make_z(2, 0, S)
+        gained_scores(3)
+        quantise_w("w2", 0, buffer([P, P], U32, "q_w2_0", "q_w2_0"))
+        quantise_w("w1", 0, buffer([P, P], U32, "q_w1_0", "q_w1_0"))
+        make_z(3, 0, S_HALF)
+        round_z(0)
+        make_z(3, S_HALF, S)
+        quantise_z(0)
+        round_z(1)
+        quantise_z(1)
+        last_fetch = "at_n2_%d_%d" % (PACK - 1, S_HALF)
+        round_w("w2", 1, nc.scalar.copy, buffer([P, P * PACK], BF16, "bf_w2_1", last_fetch))
+        round_w("w1", 1, nc.scalar.copy, buffer([P, P * PACK], BF16, "bf_w1_1", "gs"))
 
-        z32 = tagged([P, PACK, S], F32, "z32", "z32")
-        z_bf = turn.tile([P, S * PACK], BF16, name="z_bf", offset=1536, align_bytes=64)
-        z_q = pool.tile([P, S], U32, name="z_q", align_bytes=64)
-        z_sc = pool.tile([P, S], U8, name="z_sc", align_bytes=64)
-        gs = tagged([P, PACK, S], F32, "gs", "gs")
+        def product(m, c0, c1, copy, bank):
+            acc = psum.tile([P, c1 - c0], F32, name="h_ps%d_%d" % (m, c0), tag=bank)
+            nc.tensor.matmul_mx(
+                out=acc[:], lhsT=w_q[("w2", m)][:].bitcast(FP8X4), lhsT_scale=w_sc[("w2", m)][:],
+                rhs=x2_w[:, c0:c1].bitcast(FP8X4), rhs_scale=x2_sc[:, c0:c1], start=True, stop=False,
+            )
+            nc.tensor.matmul_mx(
+                out=acc[:], lhsT=w_q[("w1", m)][:].bitcast(FP8X4), lhsT_scale=w_sc[("w1", m)][:],
+                rhs=z_q[:, c0:c1].bitcast(FP8X4), rhs_scale=z_sc[:, c0:c1], start=False, stop=True,
+            )
+            copy(h[m][:, c0:c1], acc[:])
 
-        def fetch(t, c0, c1):
-            a = tagged([P, c1 - c0], F32, "a%d_%d" % (t, c0), "a%d_%d" % (t, c0))
-            b = tagged([P, c1 - c0], F32, "b%d_%d" % (t, c0), "b%d_%d" % (t, c0))
-            low = tagged([P, c1 - c0], F32, "low%d_%d" % (t, c0), "low%d_%d" % (t, c0))
-            nc.scalar.activation(a[:], s[t][:].indirect(n1_t[:, c0 // 16:c1 // 16]), COPY)
-            nc.scalar.activation(b[:], s[t][:].indirect(n2_t[:, c0 // 16:c1 // 16]), COPY)
-            nc.vector.tensor_tensor(low[:], a[:], b[:], ALU.min)
-            nc.vector.scalar_tensor_tensor(z32[:, t, c0:c1], low[:], neg_g[:, t:t + 1], gs[:, t, c0:c1], ALU.mult, ALU.add)
+        product(0, 0, S_HALF, nc.scalar.copy, "s_ps0")
+        product(0, S_HALF, S, nc.scalar.copy, "h_ps0")
+        bf_w2_2 = after_z.tile([P, P * PACK], BF16, name="bf_w2_2", offset=bf_bytes, align_bytes=64)
+        q_w2_1 = after_z.tile([P, P], U32, name="q_w2_1", offset=2 * bf_bytes, align_bytes=64)
+        q_w1_1 = after_z.tile([P, P], U32, name="q_w1_1", offset=2 * bf_bytes + q_bytes, align_bytes=64)
+        bf_w1_2 = after_z.tile([P, P * PACK], BF16, name="bf_w1_2", offset=2 * bf_bytes + 2 * q_bytes, align_bytes=64)
+        round_w("w2", 2, nc.vector.tensor_copy, bf_w2_2)
+        round_w("w1", 2, nc.vector.tensor_copy, bf_w1_2)
+        quantise_w("w2", 1, q_w2_1)
+        quantise_w("w1", 1, q_w1_1)
+        product(1, 0, S, nc.vector.tensor_copy, "h_ps1")
+        quantise_w("w2", 2, buffer([P, P], U32, "q_w2_2", "q_w2_2"))
+        quantise_w("w1", 2, buffer([P, P], U32, "q_w1_2", "q_w1_2"))
+        product(2, 0, S, nc.vector.tensor_copy, "h_ps2")
+        round_w("w2", 3, nc.vector.tensor_copy, buffer([P, P * PACK], BF16, "bf_w2_3", last_fetch))
+        round_w("w1", 3, nc.vector.tensor_copy, buffer([P, P * PACK], BF16, "bf_w1_3", "gs"))
+        quantise_w("w2", 3, buffer([P, P], U32, "q_w2_3", "q_w2_3"))
+        quantise_w("w1", 3, buffer([P, P], U32, "q_w1_3", "q_w1_3"))
+        product(3, 0, S, nc.vector.tensor_copy, "h_ps3")
 
-        def round_z(c0, c1):
-            nc.vector.tensor_copy(z_bf[:, c0 * PACK:c1 * PACK].rearrange("p (c i t) -> p c t i", i=4, t=PACK),
-                                  z32[:, :, c0:c1].rearrange("p t (c i) -> p c t i", i=4))
-
-        def quant_z(c0, c1):
-            nc.vector.quantize_mx(out=z_q[:, c0:c1].bitcast(FP8X4), scales=z_sc[:, c0:c1], in_=z_bf[:, c0 * PACK:c1 * PACK])
-
-        for t in range(PACK):
-            nc.vector.tensor_scalar(gs[:, t, :], s[t][:, :S], g[:, t:t + 1], None, ALU.mult)
-        for t in range(PACK):
-            fetch(t, 0, S)
-        cast_w("w2", 0, P, nc.scalar.copy, tagged([P, P * PACK], BF16, "bf_w2_0", "a0_0"))
-        cast_w("w1", 0, P, nc.scalar.copy, tagged([P, P * PACK], BF16, "bf_w1_0", "b0_0"))
-        cast_w("w2", P, 2 * P, nc.scalar.copy, tagged([P, P * PACK], BF16, "bf_w2_1", "b3_0"))
-        cast_w("w1", P, 2 * P, nc.scalar.copy, tagged([P, P * PACK], BF16, "bf_w1_1", "gs"))
-        round_z(0, S)
-        quant_w("w2", 0, P, tagged([P, P], U32, "q_w2_0", "low3_0"))
-        quant_z(0, S)
-        quant_w("w1", 0, P, tagged([P, P], U32, "q_w1_0", "z32"))
-
-        h_ps = [psum.tile([P, S], F32, name="h_ps%d" % m) for m in range(4)]
-
-        def product(m, copy):
-            nc.tensor.matmul_mx(out=h_ps[m][:], lhsT=w_q[("w2", m)], lhsT_scale=w_sc[("w2", m)],
-                                rhs=x2_w[:].bitcast(FP8X4), rhs_scale=x2_sc[:], start=True, stop=False)
-            nc.tensor.matmul_mx(out=h_ps[m][:], lhsT=w_q[("w1", m)], lhsT_scale=w_sc[("w1", m)],
-                                rhs=z_q[:].bitcast(FP8X4), rhs_scale=z_sc[:], start=False, stop=True)
-            copy(h[m][:, :S], h_ps[m][:])
-
-        def members(m, pieces):
+        for m in range(TILES):
             mb = pool.tile([P, J], F32, name="mb%d" % m)
             mx = pool.tile([P, S], F32, name="mx%d" % m)
-            for c0, c1 in pieces:
-                nc.scalar.activation(mb[:, 2 * c0:2 * c1], h[m][:].indirect(n3_t[:, c0 // 8:c1 // 8]), COPY)
-                nc.vector.tensor_tensor(mx[:, c0:c1], mb[:, 2 * c0:2 * c1:2], mb[:, 2 * c0 + 1:2 * c1:2], ALU.max)
-                nc.vector.tensor_tensor(st[m][:, c0:c1], h[m][:, c0:c1], mx[:, c0:c1], ALU.subtract)
+            nc.scalar.activation(mb[:], h[m][:].indirect(n3_t[:]), COPY)
+            nc.vector.tensor_tensor(mx[:], mb[:, 0:J:2], mb[:, 1:J:2], ALU.max)
+            nc.vector.tensor_tensor(st[m][:, :S], h[m][:, :S], mx[:], ALU.subtract)
 
-        def finish(m, pieces):
+        for m in range(TILES):
+            pieces = [(0, S)] if m < TILES - 1 else [(0, LAST_CUT), (LAST_CUT, S)]
             for c0, c1 in pieces:
-                far = pool.tile([P, c1 - c0], F32, name="far%d_%d" % (m, c0))
+                at_n4 = pool.tile([P, c1 - c0], F32, name="at_n4_%d_%d" % (m, c0))
                 res = pool.tile([P, c1 - c0], F32, name="res%d_%d" % (m, c0))
-                nc.scalar.activation(far[:], st[m][:].indirect(n4_t[:, c0 // 16:c1 // 16]), COPY)
-                nc.vector.tensor_tensor(res[:], st[m][:, c0:c1], far[:], ALU.max)
+                nc.scalar.activation(at_n4[:], st[m][:].indirect(n4_t[:, c0 // 16:c1 // 16]), COPY)
+                nc.vector.tensor_tensor(res[:], st[m][:, c0:c1], at_n4[:], ALU.max)
                 nc.sync.dma_start(out[m * P:(m + 1) * P, c0:c1], res[:])
-
-        whole = [(0, S)]
-        product(0, nc.scalar.copy)
-        cast_w("w2", 2 * P, 3 * P, nc.vector.tensor_copy, turn.tile([P, P * PACK], BF16, name="bf_w2_2", offset=1024, align_bytes=64))
-        cast_w("w1", 2 * P, 3 * P, nc.vector.tensor_copy, turn.tile([P, P * PACK], BF16, name="bf_w1_2", offset=3072, align_bytes=64))
-        quant_w("w2", P, 2 * P, turn.tile([P, P], U32, name="q_w2_1", offset=2048, align_bytes=64))
-        quant_w("w1", P, 2 * P, turn.tile([P, P], U32, name="q_w1_1", offset=2560, align_bytes=64))
-        product(1, nc.vector.tensor_copy)
-        quant_w("w2", 2 * P, 3 * P, tagged([P, P], U32, "q_w2_2", "q_w2_2"))
-        quant_w("w1", 2 * P, 3 * P, tagged([P, P], U32, "q_w1_2", "q_w1_2"))
-        product(2, nc.vector.tensor_copy)
-        cast_w("w2", 3 * P, N, nc.vector.tensor_copy, tagged([P, P * PACK], BF16, "bf_w2_3", "b3_0"))
-        cast_w("w1", 3 * P, N, nc.vector.tensor_copy, tagged([P, P * PACK], BF16, "bf_w1_3", "gs"))
-        quant_w("w2", 3 * P, N, tagged([P, P], U32, "q_w2_3", "q_w2_3"))
-        quant_w("w1", 3 * P, N, tagged([P, P], U32, "q_w1_3", "q_w1_3"))
-        product(3, nc.vector.tensor_copy)
-        for m in range(4):
-            members(m, whole)
-        for m in range(3):
-            finish(m, whole)
-        finish(3, [(0, 192), (192, S)])

from contextlib import ExitStack

import concourse.mybir as mybir

F32 = mybir.dt.float32
BF16 = mybir.dt.bfloat16
I32 = mybir.dt.int32
U32 = mybir.dt.uint32
U16 = mybir.dt.uint16
U8 = mybir.dt.uint8
FP8X4 = mybir.dt.float8_e4m3fn_x4
ALU = mybir.AluOpType
COPY = mybir.ActivationFunctionType.Copy

P = 128
PACK = 4
T = 2048
S = 256
H = 512
N = 512
J = 512
TILES = N // P
W_HALF = N // 2
S_HALF = S // 2
LAST_CUT = 192
SPARE = 16
SCORE_FACTOR = 0.0625
FLOPS = 3 * 2 * 512 * 512 * S


def tile_picked_kmixunderghopm_none_p_kernel(
    tc, x_words, x_scales, d_words, d_scales, gn, w1, w2, offs, k1, n1, n2, two, n3, n4, out
):
    nc = tc.nc
    with ExitStack() as ctx:
        lists = ctx.enter_context(tc.tile_pool(name="lists", bufs=1))
        pool = ctx.enter_context(tc.tile_pool(name="pool", bufs=1))
        after_z = ctx.enter_context(tc.tile_pool(name="after_z", bufs=1))
        psum = ctx.enter_context(tc.psum_pool(name="psum", bufs=1))

        def load_list(src, name):
            tile = lists.tile(list(src.shape), U16, name=name)
            nc.sync.dma_start(tile[:], src)
            return tile

        def buffer(shape, dtype, name, tag):
            return pool.tile(shape, dtype, name=name, tag=tag, align_bytes=64)

        d_sc = pool.tile([P, T], U8, name="d_sc", align_bytes=64)
        x_sc = pool.tile([P, T], U8, name="x_sc", align_bytes=64)
        nc.vector.memset(d_sc[:, :T // 2].bitcast(I32), 0)
        nc.gpsimd.memset(d_sc[:, T // 2:].bitcast(I32), 0)
        nc.vector.memset(x_sc[:].bitcast(I32), 0)

        s = [pool.tile([P, S + SPARE], F32, name="s%d" % t) for t in range(PACK)]
        h = [pool.tile([P, J + SPARE], F32, name="h%d" % m) for m in range(TILES)]
        st = [pool.tile([P, S + SPARE], F32, name="st%d" % m) for m in range(TILES)]
        for windows in zip(s, h, st):
            for window in windows:
                nc.vector.memset(window[:, S:], 0.0)

        k1_t = load_list(k1, "k1")
        offs_t = load_list(offs, "offs")
        n1_t = load_list(n1, "n1")
        for e in range(2):
            nc.sync.dma_start(d_sc[e:P:16, :].bitcast(I32), d_scales[0, e:16:2, :].bitcast(I32))
        d_w = buffer([P, T], U32, "d_w", "d_w")
        nc.sync.dma_start(d_w[:].bitcast(I32), d_words[0].rearrange("p n t -> p (n t)").bitcast(I32))
        for a in range(4):
            nc.sync.dma_start(x_sc[a:P:32, :].bitcast(I32), x_scales[0, a:16:4, :].bitcast(I32))
        x_w = buffer([P, T], U32, "x_w", "x_w")
        nc.sync.dma_start(x_w[:].bitcast(I32), x_words[0].rearrange("p n t -> p (n t)").bitcast(I32))
        gain = pool.tile([P, PACK], F32, name="gain")
        nc.sync.dma_start(gain[:], gn.rearrange("(p t) o -> p (t o)", t=PACK))
        n2_t = load_list(n2, "n2")

        dk_sc = buffer([P, H], U8, "dk_sc", "dk_sc")
        nc.vector.tensor_copy(dk_sc[:], d_sc[:].indirect(k1_t[:]))
        key_sc = buffer([P, H], U8, "key_sc", "key_sc")
        nc.vector.tensor_copy(
            key_sc[:].rearrange("p (t m) -> p m t", t=PACK), dk_sc[:].rearrange("p (m t) -> p m t", t=PACK)
        )
        nc.sync.dma_start(key_sc[2:P:32, :].bitcast(I32), key_sc[16:P:32, :].bitcast(I32))
        two_t = load_list(two, "two")
        nc.sync.dma_start(key_sc[3:P:32, :].bitcast(I32), key_sc[17:P:32, :].bitcast(I32))

        w_raw = {}
        for half in range(2):
            for name, w in (("w2", w2), ("w1", w1)):
                raw = pool.tile([P, PACK, W_HALF], F32, name="raw_%s_%d" % (name, half))
                rows = w.rearrange("(p j) n -> p j n", j=PACK)
                nc.sync.dma_start(raw[:], rows[:, :, half * W_HALF:(half + 1) * W_HALF])
                w_raw[(name, half)] = raw
        n3_t = load_list(n3, "n3")
        n4_t = load_list(n4, "n4")

        xq_sc = buffer([P, S], U8, "xq_sc", "xq_sc")
        x2_sc = buffer([P, S], U8, "x2_sc", "x2_sc")
        dk_w = buffer([P, H], U32, "dk_w", "dk_w")
        key_w = buffer([P, H], U32, "key_w", "key_w")
        xq_w = buffer([P, S], U32, "xq_w", "xq_w")
        x2_w = buffer([P, S], U32, "x2_w", "x2_w")
        nc.vector.tensor_copy(dk_w[:], d_w[:].indirect(k1_t[:]))
        nc.vector.tensor_copy(
            key_w[:].rearrange("p (t m) -> p m t", t=PACK), dk_w[:].rearrange("p (m t) -> p m t", t=PACK)
        )
        nc.vector.tensor_copy(xq_sc[:], x_sc[:].indirect(offs_t[:]))
        nc.vector.tensor_copy(xq_w[:], x_w[:].indirect(offs_t[:]))

        s_ps = [psum.tile([P, S], F32, name="s_ps%d" % t, tag="s_ps%d" % t) for t in range(PACK)]
        for t in range(PACK):
            cols = slice(t * P, (t + 1) * P)
            nc.tensor.matmul_mx(
                out=s_ps[t][:], lhsT=key_w[:, cols].bitcast(FP8X4), lhsT_scale=key_sc[:, cols],
                rhs=xq_w[:].bitcast(FP8X4), rhs_scale=xq_sc[:], start=True, stop=True,
            )
        neg_gain = pool.tile([P, PACK], F32, name="neg_gain")
        nc.vector.tensor_scalar(neg_gain[:], gain[:], -1.0, None, ALU.mult)
        nc.scalar.activation(s[0][:, :S], s_ps[0][:], COPY, scale=SCORE_FACTOR)
        nc.vector.tensor_copy(x2_sc[:], x_sc[:].indirect(two_t[:]))
        for t in range(1, PACK):
            nc.vector.tensor_scalar(s[t][:, :S], s_ps[t][:], SCORE_FACTOR, None, ALU.mult)

        w_bf, w_q, w_sc = {}, {}, {}

        def round_w(name, m, copy, grouped):
            c0 = m * P % W_HALF
            src = w_raw[(name, m * P // W_HALF)][:, :, c0:c0 + P]
            copy(
                grouped[:].rearrange("p (c i t) -> p c t i", i=4, t=PACK), src.rearrange("p t (c i) -> p c t i", i=4)
            )
            w_bf[(name, m)] = grouped

        def quantise_w(name, m, codes):
            scales = pool.tile([P, P], U8, name="sc_%s_%d" % (name, m), align_bytes=64)
            nc.vector.quantize_mx(out=codes[:].bitcast(FP8X4), scales=scales[:], in_=w_bf[(name, m)][:])
            w_q[(name, m)], w_sc[(name, m)] = codes, scales

        bf_bytes, q_bytes = 2 * P * PACK, 4 * P
        z_bf_at = bf_bytes + q_bytes
        z32 = pool.tile([P, 2, PACK, S_HALF], F32, name="z32")
        z_bf = after_z.tile([P, S * PACK], BF16, name="z_bf", offset=z_bf_at, align_bytes=64)
        z_q = buffer([P, S], U32, "z_q", "z_q")
        z_sc = buffer([P, S], U8, "z_sc", "z_sc")
        gs = buffer([P, PACK, S], F32, "gs", "gs")

        def gained_scores(t):
            nc.vector.tensor_scalar(gs[:, t, :], s[t][:, :S], gain[:, t:t + 1], None, ALU.mult)

        def make_z(t, c0, c1):
            at_n1, at_n2, low = (
                buffer([P, c1 - c0], F32, "%s%d_%d" % (role, t, c0), "%s%d_%d" % (role, t, c0))
                for role in ("at_n1_", "at_n2_", "low_")
            )
            nc.scalar.activation(at_n1[:], s[t][:].indirect(n1_t[:, c0 // 16:c1 // 16]), COPY)
            nc.scalar.activation(at_n2[:], s[t][:].indirect(n2_t[:, c0 // 16:c1 // 16]), COPY)
            nc.vector.tensor_tensor(low[:], at_n1[:], at_n2[:], ALU.min)
            nc.vector.scalar_tensor_tensor(
                z32[:, c0 // S_HALF:c1 // S_HALF, t, :], low[:].rearrange("p (u j) -> p u j", j=S_HALF),
                neg_gain[:, t:t + 1], gs[:, t, c0:c1].rearrange("p (u j) -> p u j", j=S_HALF), ALU.mult, ALU.add,
            )

        def round_z(half):
            dst = z_bf[:, half * S_HALF * PACK:(half + 1) * S_HALF * PACK]
            nc.vector.tensor_copy(
                dst.rearrange("p (c i t) -> p c t i", i=4, t=PACK),
                z32[:, half, :, :].rearrange("p t (c i) -> p c t i", i=4),
            )

        def quantise_z(half):
            cols = slice(half * S_HALF, (half + 1) * S_HALF)
            src = z_bf[:, half * S_HALF * PACK:(half + 1) * S_HALF * PACK]
            nc.vector.quantize_mx(out=z_q[:, cols].bitcast(FP8X4), scales=z_sc[:, cols], in_=src)

        gained_scores(0)
        nc.vector.tensor_copy(x2_w[:], x_w[:].indirect(two_t[:]))
        make_z(0, 0, S)
        gained_scores(1)
        round_w("w2", 0, nc.vector.tensor_copy, buffer([P, P * PACK], BF16, "bf_w2_0", "bf_w2_0"))
        make_z(1, 0, S)
        gained_scores(2)
        round_w("w1", 0, nc.vector.tensor_copy, buffer([P, P * PACK], BF16, "bf_w1_0", "bf_w1_0"))
        make_z(2, 0, S)
        gained_scores(3)
        quantise_w("w2", 0, buffer([P, P], U32, "q_w2_0", "q_w2_0"))
        quantise_w("w1", 0, buffer([P, P], U32, "q_w1_0", "q_w1_0"))
        make_z(3, 0, S_HALF)
        round_z(0)
        make_z(3, S_HALF, S)
        quantise_z(0)
        round_z(1)
        quantise_z(1)
        last_fetch = "at_n2_%d_%d" % (PACK - 1, S_HALF)
        round_w("w2", 1, nc.scalar.copy, buffer([P, P * PACK], BF16, "bf_w2_1", last_fetch))
        round_w("w1", 1, nc.scalar.copy, buffer([P, P * PACK], BF16, "bf_w1_1", "gs"))

        def product(m, c0, c1, copy, bank):
            acc = psum.tile([P, c1 - c0], F32, name="h_ps%d_%d" % (m, c0), tag=bank)
            nc.tensor.matmul_mx(
                out=acc[:], lhsT=w_q[("w2", m)][:].bitcast(FP8X4), lhsT_scale=w_sc[("w2", m)][:],
                rhs=x2_w[:, c0:c1].bitcast(FP8X4), rhs_scale=x2_sc[:, c0:c1], start=True, stop=False,
            )
            nc.tensor.matmul_mx(
                out=acc[:], lhsT=w_q[("w1", m)][:].bitcast(FP8X4), lhsT_scale=w_sc[("w1", m)][:],
                rhs=z_q[:, c0:c1].bitcast(FP8X4), rhs_scale=z_sc[:, c0:c1], start=False, stop=True,
            )
            copy(h[m][:, c0:c1], acc[:])

        product(0, 0, S_HALF, nc.scalar.copy, "s_ps0")
        product(0, S_HALF, S, nc.scalar.copy, "h_ps0")
        bf_w2_2 = after_z.tile([P, P * PACK], BF16, name="bf_w2_2", offset=bf_bytes, align_bytes=64)
        q_w2_1 = after_z.tile([P, P], U32, name="q_w2_1", offset=2 * bf_bytes, align_bytes=64)
        q_w1_1 = after_z.tile([P, P], U32, name="q_w1_1", offset=2 * bf_bytes + q_bytes, align_bytes=64)
        bf_w1_2 = after_z.tile([P, P * PACK], BF16, name="bf_w1_2", offset=2 * bf_bytes + 2 * q_bytes, align_bytes=64)
        round_w("w2", 2, nc.vector.tensor_copy, bf_w2_2)
        round_w("w1", 2, nc.vector.tensor_copy, bf_w1_2)
        quantise_w("w2", 1, q_w2_1)
        quantise_w("w1", 1, q_w1_1)
        product(1, 0, S, nc.vector.tensor_copy, "h_ps1")
        quantise_w("w2", 2, buffer([P, P], U32, "q_w2_2", "q_w2_2"))
        quantise_w("w1", 2, buffer([P, P], U32, "q_w1_2", "q_w1_2"))
        product(2, 0, S, nc.vector.tensor_copy, "h_ps2")
        round_w("w2", 3, nc.vector.tensor_copy, buffer([P, P * PACK], BF16, "bf_w2_3", last_fetch))
        round_w("w1", 3, nc.vector.tensor_copy, buffer([P, P * PACK], BF16, "bf_w1_3", "gs"))
        quantise_w("w2", 3, buffer([P, P], U32, "q_w2_3", "q_w2_3"))
        quantise_w("w1", 3, buffer([P, P], U32, "q_w1_3", "q_w1_3"))
        product(3, 0, S, nc.vector.tensor_copy, "h_ps3")

        for m in range(TILES):
            mb = pool.tile([P, J], F32, name="mb%d" % m)
            mx = pool.tile([P, S], F32, name="mx%d" % m)
            nc.scalar.activation(mb[:], h[m][:].indirect(n3_t[:]), COPY)
            nc.vector.tensor_tensor(mx[:], mb[:, 0:J:2], mb[:, 1:J:2], ALU.max)
            nc.vector.tensor_tensor(st[m][:, :S], h[m][:, :S], mx[:], ALU.subtract)

        for m in range(TILES):
            pieces = [(0, S)] if m < TILES - 1 else [(0, LAST_CUT), (LAST_CUT, S)]
            for c0, c1 in pieces:
                at_n4 = pool.tile([P, c1 - c0], F32, name="at_n4_%d_%d" % (m, c0))
                res = pool.tile([P, c1 - c0], F32, name="res%d_%d" % (m, c0))
                nc.scalar.activation(at_n4[:], st[m][:].indirect(n4_t[:, c0 // 16:c1 // 16]), COPY)
                nc.vector.tensor_tensor(res[:], st[m][:, c0:c1], at_n4[:], ALU.max)
                nc.sync.dma_start(out[m * P:(m + 1) * P, c0:c1], res[:])
